import numpy as np
import ml_dtypes

BF16 = ml_dtypes.bfloat16


def bf(x):
    return np.asarray(x, np.float32).astype(BF16)


def f32(x):
    return np.asarray(x, np.float32)


def f64(x):
    return np.asarray(x).astype(np.float64)


def striped(idx):
    return np.concatenate([l.reshape(-1, 16).T for l in idx])


def rows(idx, k):
    return np.tile(np.repeat(idx, 16, axis=0), (k // (16 * 8), 1))


def look(tab, idx):
    return np.take_along_axis(f64(tab), rows(idx, len(tab)), axis=1)


K, S, V, N, M = 256, 2048, 1024, 1024, 256


def setup_inputs():
    return {"tab": f32(np.random.standard_normal((2, K, S))), "w": bf(np.random.standard_normal((K, M)) / np.sqrt(K)), "b": f32(0.5 * np.random.standard_normal((M, 1))), "offs": striped(np.stack([np.random.permutation(S)[:N] for _ in range(8)]))}


def reference(tab, w, b, offs):
    idx = np.stack([g.T.reshape(-1) for g in np.split(offs, 8)])
    x = (np.minimum(np.maximum(look(tab[0], idx), -1.25), 1.0)) * (np.tanh(look(tab[1], idx)))
    return np.maximum(f64(w).T @ x + f64(b), 0.0)

@@ -1,0 +1,72 @@
+import concourse.mybir as mybir
+
+F32, BF16, U16 = mybir.dt.float32, mybir.dt.bfloat16, mybir.dt.uint16
+ALU = mybir.AluOpType
+ACT = mybir.ActivationFunctionType
+
+P = 128
+K, S, N, M = 256, 2048, 1024, 256
+HALF = 512
+COLS = HALF // 16
+KB, MB, HALVES = K // P, M // P, N // HALF
+
+LOW, HIGH = -1.25, 1.0
+
+FLOPS = 2 * K * M * N
+
+
+def tile_lookup_vg_cliptanh_relu_kernel(tc, tab, w, b, offs, out):
+    nc = tc.nc
+    with (
+        tc.tile_pool(name="held", bufs=1) as held,
+        tc.psum_pool(name="psum", bufs=1) as psum,
+    ):
+        offsets = held.tile([P, N // 16], U16, name="offsets")
+        nc.sync.dma_start(offsets[:], offs)
+        values = [held.tile([P, S], F32, name=f"values{k}") for k in range(KB)]
+        gates = [held.tile([P, S], F32, name=f"gates{k}") for k in range(KB)]
+        weights = [held.tile([P, M], BF16, name=f"weights{k}") for k in range(KB)]
+        bias = [held.tile([P, 1], F32, name=f"bias{m}") for m in range(MB)]
+        for k in range(KB):
+            rows = slice(k * P, (k + 1) * P)
+            nc.sync.dma_start(values[k][:], tab[0, rows, :])
+            nc.sync.dma_start(gates[k][:], tab[1, rows, :])
+            nc.gpsimd.dma_start(weights[k][:], w[rows, :])
+        with nc.allow_non_contiguous_dma(reason="one bias to a partition"):
+            for m in range(MB):
+                nc.gpsimd.dma_start(bias[m][:], b[m * P : (m + 1) * P, :])
+
+        sums = [
+            [psum.tile([P, HALF], F32, name=f"sums{m}_{h}") for h in range(HALVES)]
+            for m in range(MB)
+        ]
+
+        for k in range(KB):
+            clamped = [held.tile([P, HALF], F32, name=f"clamped{k}_{h}") for h in range(HALVES)]
+            opened = [held.tile([P, HALF], F32, name=f"opened{k}_{h}") for h in range(HALVES)]
+            for h in range(HALVES):
+                part = offsets[:, h * COLS : (h + 1) * COLS]
+                nc.vector.tensor_scalar(
+                    clamped[h][:], values[k][:].indirect(part), LOW, HIGH, ALU.max, ALU.min
+                )
+                nc.scalar.activation(opened[h][:], gates[k][:].indirect(part), ACT.Tanh)
+            for h in range(HALVES):
+                x = held.tile([P, HALF], BF16, name=f"x{k}_{h}")
+                nc.vector.tensor_tensor(x[:], clamped[h][:], opened[h][:], ALU.mult)
+                for m in range(MB):
+                    nc.tensor.matmul(
+                        sums[m][h][:],
+                        weights[k][:, m * P : (m + 1) * P],
+                        x[:],
+                        start=k == 0,
+                        stop=k == KB - 1,
+                    )
+
+        for h in range(HALVES):
+            cols = slice(h * HALF, (h + 1) * HALF)
+            lower = held.tile([P, HALF], F32, name=f"lower{h}")
+            nc.vector.tensor_scalar(lower[:], sums[0][h][:], bias[0][:], 0.0, ALU.add, ALU.max)
+            nc.sync.dma_start(out[0:P, cols], lower[:])
+            upper = held.tile([P, HALF], F32, name=f"upper{h}")
+            nc.scalar.activation(upper[:], sums[1][h][:], ACT.Relu, bias=bias[1][:])
+            nc.sync.dma_start(out[P:M, cols], upper[:])

@@ -30,11 +30,11 @@ def tile_lookup_vg_cliptanh_relu_kernel(tc, tab, w, b, offs, out):
         for k in range(KB):
             rows = slice(k * P, (k + 1) * P)
             nc.sync.dma_start(values[k][:], tab[0, rows, :])
+            nc.sync.dma_start(weights[k][:], w[rows, :])
             nc.sync.dma_start(gates[k][:], tab[1, rows, :])
-            nc.gpsimd.dma_start(weights[k][:], w[rows, :])
         with nc.allow_non_contiguous_dma(reason="one bias to a partition"):
             for m in range(MB):
-                nc.gpsimd.dma_start(bias[m][:], b[m * P : (m + 1) * P, :])
+                nc.sync.dma_start(bias[m][:], b[m * P : (m + 1) * P, :])
 
         sums = [
             [psum.tile([P, HALF], F32, name=f"sums{m}_{h}") for h in range(HALVES)]

@@ -25,13 +25,13 @@ def tile_lookup_vg_cliptanh_relu_kernel(tc, tab, w, b, offs, out):
         nc.sync.dma_start(offsets[:], offs)
         values = [held.tile([P, S], F32, name=f"values{k}") for k in range(KB)]
         gates = [held.tile([P, S], F32, name=f"gates{k}") for k in range(KB)]
-        weights = [held.tile([P, M], BF16, name=f"weights{k}") for k in range(KB)]
+        weights = held.tile([P, KB, M], BF16, name="weights")
         bias = [held.tile([P, 1], F32, name=f"bias{m}") for m in range(MB)]
         for k in range(KB):
             rows = slice(k * P, (k + 1) * P)
             nc.sync.dma_start(values[k][:], tab[0, rows, :])
-            nc.sync.dma_start(weights[k][:], w[rows, :])
             nc.sync.dma_start(gates[k][:], tab[1, rows, :])
+        nc.sync.dma_start(weights[:], w.rearrange("(k p) m -> p k m", p=P))
         with nc.allow_non_contiguous_dma(reason="one bias to a partition"):
             for m in range(MB):
                 nc.sync.dma_start(bias[m][:], b[m * P : (m + 1) * P, :])
@@ -56,7 +56,7 @@ def tile_lookup_vg_cliptanh_relu_kernel(tc, tab, w, b, offs, out):
                 for m in range(MB):
                     nc.tensor.matmul(
                         sums[m][h][:],
-                        weights[k][:, m * P : (m + 1) * P],
+                        weights[:, k, m * P : (m + 1) * P],
                         x[:],
                         start=k == 0,
                         stop=k == KB - 1,

@@ -7,8 +7,9 @@ ACT = mybir.ActivationFunctionType
 P = 128
 K, S, N, M = 256, 2048, 1024, 256
 HALF = 512
+QUARTER = 256
 COLS = HALF // 16
-KB, MB, HALVES = K // P, M // P, N // HALF
+KB, MB, HALVES, QUARTERS = K // P, M // P, N // HALF, N // QUARTER
 
 LOW, HIGH = -1.25, 1.0
 
@@ -37,36 +38,38 @@ def tile_lookup_vg_cliptanh_relu_kernel(tc, tab, w, b, offs, out):
                 nc.sync.dma_start(bias[m][:], b[m * P : (m + 1) * P, :])
 
         sums = [
-            [psum.tile([P, HALF], F32, name=f"sums{m}_{h}") for h in range(HALVES)]
+            [psum.tile([P, QUARTER], F32, name=f"sums{m}_{q}") for q in range(QUARTERS)]
             for m in range(MB)
         ]
 
         for k in range(KB):
-            clamped = [held.tile([P, HALF], F32, name=f"clamped{k}_{h}") for h in range(HALVES)]
-            opened = [held.tile([P, HALF], F32, name=f"opened{k}_{h}") for h in range(HALVES)]
+            clamped = held.tile([P, N], F32, name=f"clamped{k}")
+            opened = held.tile([P, N], F32, name=f"opened{k}")
             for h in range(HALVES):
                 part = offsets[:, h * COLS : (h + 1) * COLS]
+                cols = slice(h * HALF, (h + 1) * HALF)
                 nc.vector.tensor_scalar(
-                    clamped[h][:], values[k][:].indirect(part), LOW, HIGH, ALU.max, ALU.min
+                    clamped[:, cols], values[k][:].indirect(part), LOW, HIGH, ALU.max, ALU.min
                 )
-                nc.scalar.activation(opened[h][:], gates[k][:].indirect(part), ACT.Tanh)
-            for h in range(HALVES):
-                x = held.tile([P, HALF], BF16, name=f"x{k}_{h}")
-                nc.vector.tensor_tensor(x[:], clamped[h][:], opened[h][:], ALU.mult)
+                nc.scalar.activation(opened[:, cols], gates[k][:].indirect(part), ACT.Tanh)
+            x = held.tile([P, N], BF16, name=f"x{k}")
+            for q in range(QUARTERS):
+                cols = slice(q * QUARTER, (q + 1) * QUARTER)
+                nc.vector.tensor_tensor(x[:, cols], clamped[:, cols], opened[:, cols], ALU.mult)
                 for m in range(MB):
                     nc.tensor.matmul(
-                        sums[m][h][:],
+                        sums[m][q][:],
                         weights[:, k, m * P : (m + 1) * P],
-                        x[:],
+                        x[:, cols],
                         start=k == 0,
                         stop=k == KB - 1,
                     )
 
-        for h in range(HALVES):
-            cols = slice(h * HALF, (h + 1) * HALF)
-            lower = held.tile([P, HALF], F32, name=f"lower{h}")
-            nc.vector.tensor_scalar(lower[:], sums[0][h][:], bias[0][:], 0.0, ALU.add, ALU.max)
+        for q in range(QUARTERS):
+            cols = slice(q * QUARTER, (q + 1) * QUARTER)
+            lower = held.tile([P, QUARTER], F32, name=f"lower{q}")
+            nc.vector.tensor_scalar(lower[:], sums[0][q][:], bias[0][:], 0.0, ALU.add, ALU.max)
             nc.sync.dma_start(out[0:P, cols], lower[:])
-            upper = held.tile([P, HALF], F32, name=f"upper{h}")
-            nc.scalar.activation(upper[:], sums[1][h][:], ACT.Relu, bias=bias[1][:])
+            upper = held.tile([P, QUARTER], F32, name=f"upper{q}")
+            nc.scalar.activation(upper[:], sums[1][q][:], ACT.Relu, bias=bias[1][:])
             nc.sync.dma_start(out[P:M, cols], upper[:])

import concourse.mybir as mybir

F32, BF16, U16 = mybir.dt.float32, mybir.dt.bfloat16, mybir.dt.uint16
ALU = mybir.AluOpType
ACT = mybir.ActivationFunctionType

P = 128
K, S, N, M = 256, 2048, 1024, 256
HALF = 512
QUARTER = 256
COLS = HALF // 16
KB, MB, HALVES, QUARTERS = K // P, M // P, N // HALF, N // QUARTER

LOW, HIGH = -1.25, 1.0

FLOPS = 2 * K * M * N


def tile_lookup_vg_cliptanh_relu_kernel(tc, tab, w, b, offs, out):
    nc = tc.nc
    with (
        tc.tile_pool(name="held", bufs=1) as held,
        tc.psum_pool(name="psum", bufs=1) as psum,
    ):
        offsets = held.tile([P, N // 16], U16, name="offsets")
        nc.sync.dma_start(offsets[:], offs)
        values = [held.tile([P, S], F32, name=f"values{k}") for k in range(KB)]
        gates = [held.tile([P, S], F32, name=f"gates{k}") for k in range(KB)]
        weights = held.tile([P, KB, M], BF16, name="weights")
        bias = [held.tile([P, 1], F32, name=f"bias{m}") for m in range(MB)]
        for k in range(KB):
            rows = slice(k * P, (k + 1) * P)
            nc.sync.dma_start(values[k][:], tab[0, rows, :])
            nc.sync.dma_start(gates[k][:], tab[1, rows, :])
        nc.sync.dma_start(weights[:], w.rearrange("(k p) m -> p k m", p=P))
        with nc.allow_non_contiguous_dma(reason="one bias to a partition"):
            for m in range(MB):
                nc.sync.dma_start(bias[m][:], b[m * P : (m + 1) * P, :])

        sums = [
            [psum.tile([P, QUARTER], F32, name=f"sums{m}_{q}") for q in range(QUARTERS)]
            for m in range(MB)
        ]

        for k in range(KB):
            clamped = held.tile([P, N], F32, name=f"clamped{k}")
            opened = held.tile([P, N], F32, name=f"opened{k}")
            for h in range(HALVES):
                part = offsets[:, h * COLS : (h + 1) * COLS]
                cols = slice(h * HALF, (h + 1) * HALF)
                nc.vector.tensor_scalar(
                    clamped[:, cols], values[k][:].indirect(part), LOW, HIGH, ALU.max, ALU.min
                )
                nc.scalar.activation(opened[:, cols], gates[k][:].indirect(part), ACT.Tanh)
            x = held.tile([P, N], BF16, name=f"x{k}")
            for q in range(QUARTERS):
                cols = slice(q * QUARTER, (q + 1) * QUARTER)
                nc.vector.tensor_tensor(x[:, cols], clamped[:, cols], opened[:, cols], ALU.mult)
                for m in range(MB):
                    nc.tensor.matmul(
                        sums[m][q][:],
                        weights[:, k, m * P : (m + 1) * P],
                        x[:, cols],
                        start=k == 0,
                        stop=k == KB - 1,
                    )

        for q in range(QUARTERS):
            cols = slice(q * QUARTER, (q + 1) * QUARTER)
            lower = held.tile([P, QUARTER], F32, name=f"lower{q}")
            nc.vector.tensor_scalar(lower[:], sums[0][q][:], bias[0][:], 0.0, ALU.add, ALU.max)
            nc.sync.dma_start(out[0:P, cols], lower[:])
            upper = held.tile([P, QUARTER], F32, name=f"upper{q}")
            nc.scalar.activation(upper[:], sums[1][q][:], ACT.Relu, bias=bias[1][:])
            nc.sync.dma_start(out[P:M, cols], upper[:])
